import numpy as np, ml_dtypes
CORES = [50,106,114,52,108,116]
N = 6
TK = 64
def setup_inputs(rng):
    x = rng.standard_normal((N, 128, TK), dtype=np.float32).astype(ml_dtypes.bfloat16); w1 = (rng.standard_normal((N, 128, 128), dtype=np.float32) / 8).astype(ml_dtypes.bfloat16)
    wa = np.concatenate(list(w1.astype(np.float64)), axis=1)
    for r in range(N):
        while True:
            near = (np.abs(wa.T @ x[r].astype(np.float64)) < 2e-4).any(axis=0)
            if not near.any(): break
            x[r][:, near] = rng.standard_normal((128, int(near.sum())), dtype=np.float32).astype(ml_dtypes.bfloat16)
    return {"x": x, "dy": rng.standard_normal((N, 128, TK), dtype=np.float32).astype(ml_dtypes.bfloat16), "w1": w1, "w2t": (rng.standard_normal((N, 128, 128), dtype=np.float32) / 8).astype(ml_dtypes.bfloat16)}
def setup_inputs_big(rng):
    d = setup_inputs(rng)
    for k in ("x", "dy", "w1", "w2t"): d[k] = (d[k].astype(np.float32) * 1024.0).astype(d[k].dtype)
    return d
def setup_inputs_small(rng):
    d = setup_inputs(rng)
    for k in ("x", "dy", "w1", "w2t"): d[k] = (d[k].astype(np.float32) * (1 / 1024.0)).astype(d[k].dtype)
    return d
def setup_inputs_apart(rng):
    d = setup_inputs(rng)
    f = (10.0 ** rng.permutation(np.linspace(-1.5, 1.5, N))).astype(np.float32).reshape(N, 1, 1)
    for k in ("x", "dy", "w1", "w2t"): d[k] = (d[k].astype(np.float32) * f).astype(d[k].dtype)
    return d
def reference(x, dy, w1, w2t):
    X, DY, W1, W2T = x.astype(np.float64), dy.astype(np.float64), w1.astype(np.float64), w2t.astype(np.float64)
    dx = np.zeros((N, 128, TK))
    for r in range(N):
        for j in range(N):
            dx[r] += W1[j] @ ((W1[j].T @ X[r] > 0) * (W2T[j].T @ DY[r]))
    return {"dx": dx.astype(ml_dtypes.bfloat16)}

@@ -1,0 +1,227 @@
+from concourse.bass import DstId, RemoteDMATransfer
+from concourse.mybir import AluOpType, ActivationFunctionType
+
+NR = 6
+TK = 64
+DM = 128
+
+SCRATCH = {
+    "xd": ("sbuf", [128, 2 * TK], "bfloat16"),
+    "xdp": ("sbuf", [128, 2 * TK], "bfloat16"),
+    "ones": ("sbuf", [128, DM], "bfloat16"),
+    "ident": ("sbuf", [128, DM], "bfloat16"),
+    "pout": ("sbuf", [128, TK], "bfloat16"),
+    "pin": ("sbuf", [128, TK], "bfloat16"),
+    "res": ("sbuf", [128, TK], "bfloat16"),
+    "zb0": ("psum", [128, 512], "float32"), "zb1": ("psum", [128, 512], "float32"),
+    "ub0": ("psum", [128, 512], "float32"), "ub1": ("psum", [128, 512], "float32"),
+    "tb0": ("psum", [128, 1024], "bfloat16"), "tb1": ("psum", [128, 1024], "bfloat16"),
+    "acco": ("psum", [128, 512], "float32"), "accp": ("psum", [128, 512], "float32"),
+}
+SEMAPHORES = ["ldw", "ldx", "fill", "idn", "sent", "axd", "apin", "spo", "sdo", "sdp", "sres", "sst"]
+for _k in range(NR):
+    SCRATCH["wb%d" % _k] = ("sbuf", [128, 2 * DM], "bfloat16")
+    SCRATCH["wt%d" % _k] = ("sbuf", [128, DM], "bfloat16")
+    SCRATCH["mk%d" % _k] = ("sbuf", [128, 2 * TK], "bfloat16")
+    SCRATCH["gg%d" % _k] = ("sbuf", [128, 2 * TK], "bfloat16")
+    SEMAPHORES += ["aw%d" % _k, "sz%d" % _k, "su%d" % _k, "st%d" % _k, "sm%d" % _k, "sg%d" % _k, "sc%d" % _k]
+
+
+def _bits(m):
+    return [i for i in range(m.bit_length()) if (m >> i) & 1]
+
+
+def _mask(es):
+    return sum(1 << i for i in es)
+
+
+def _split(es, k):
+    per = 1
+    while per * 2 * k <= len(es):
+        per *= 2
+    return [es[i * per:(i + 1) * per] for i in range(k)]
+
+
+def _plan(cores, topo):
+    n = len(cores)
+    chips = sorted(set(topo.chip(c) for c in cores))
+    on = dict((ch, [r for r in range(n) if topo.chip(cores[r]) == ch]) for ch in chips)
+
+    def far(c):
+        d = [x for x in cores if topo.chip(x) != topo.chip(c)][0]
+        return _bits(topo.mask(c, d))
+
+    def near(c, d):
+        every = _bits(topo.mask(c, d))
+        only = [e for e in every if e not in far(c)]
+        return only or every
+
+    partner = dict((r, [p for p in on[topo.chip(cores[r])] if p != r][0]) for r in range(n))
+    shared = dict((r, []) for r in range(n))
+    late = dict((r, []) for r in range(n))
+    first, relay, arrive = {}, {}, {}
+    for a in reversed(range(n)):
+        ca = cores[a]
+        straight, through = [], []
+        for ch in chips:
+            if ch == topo.chip(ca):
+                continue
+            mem = on[ch]
+            if all(topo.may_write(ca, cores[m]) for m in mem):
+                h = min(mem, key=lambda m: (len(shared[m]), topo.die(cores[m]) != topo.die(ca), m))
+                shared[h].append(a)
+                straight.append(h)
+            else:
+                through += mem
+                for m in mem:
+                    late[m].append(a)
+        calls = []
+        if through:
+            gate = cores[partner[a]]
+            es = near(ca, gate)
+            calls.append([(gate, es)])
+            arrive[(gate, a)] = len(es)
+            sh = _split(far(gate), len(through))
+            relay.setdefault(gate, []).append((a, [(cores[m], sh[i]) for i, m in enumerate(through)]))
+            for i, m in enumerate(through):
+                arrive[(cores[m], a)] = len(sh[i])
+        if straight:
+            sh = _split(far(ca), len(straight))
+            calls.append([(cores[h], sh[i]) for i, h in enumerate(straight)])
+            for i, h in enumerate(straight):
+                arrive[(cores[h], a)] = len(sh[i])
+        first[a] = calls
+    jobs = {}
+    for r in range(n):
+        me = topo.chip(cores[r])
+        sh = sorted(shared[r], key=lambda a: (not topo.same_plane(topo.chip(cores[a]), me), a))
+        jobs[r] = [(r, True)] + [(a, True) for a in sh] + [(a, False) for a in sorted(late[r])]
+    return {"jobs": jobs, "first": first, "relay": relay, "arrive": arrive, "partner": partner, "near": near}
+
+
+def rank_program(g, core, T, topo):
+    cores = list(T.cores)
+    P = _plan(cores, topo)
+    S = T.sem
+    r = T.rank_of(core)
+    duties = P["relay"].get(core, [])
+    if r is None and not duties:
+        return
+    total = [0]
+
+    def push(src, dst, sem, targets):
+        if len(targets) == 1:
+            d, es = targets[0]
+            rid, pid, se = topo.addr(d)
+            g.remote_dma(out_ap=dst, in_ap=src, remote_sem=sem, local_sem=S.sent, pid=pid, routing_id=rid,
+                         dma_engine_mask=_mask(es))
+        else:
+            trs = []
+            for d, es in targets:
+                rid, pid, se = topo.addr(d)
+                trs.append(RemoteDMATransfer(dst_ids=[DstId(rid=rid, pnc=pid)], dma_engine_mask=_mask(es),
+                                             remote_sem=sem, src=src, dst=dst))
+            g.remote_dma_fused(trs, local_sem=S.sent)
+        total[0] += sum(len(es) for d, es in targets)
+
+    def pass_on():
+        for a, targets in duties:
+            g.wait_ge(S["aw%d" % a], P["arrive"][(core, a)])
+            buf = T["wb%d" % a]
+            push(buf[:], buf[:], S["aw%d" % a], targets)
+
+    if r is None:
+        pass_on()
+        g.wait_ge(S.sent, total[0])
+        return
+
+    own = T["wb%d" % r]
+    mate = cores[P["partner"][r]]
+    jobs = P["jobs"][r]
+    n = len(jobs)
+    nb = len([1 for a, both in jobs if both])
+
+    g.sync.dma_start(own[:, 0:DM], T.w1[:]).then_inc(S.ldw, 16)
+    g.scalar.dma_start(own[:, DM:2 * DM], T.w2t[:]).then_inc(S.ldw, 16)
+    g.sync.dma_start(T.xd[:, 0:TK], T.x[:]).then_inc(S.ldx, 16)
+    g.scalar.dma_start(T.xd[:, TK:2 * TK], T.dy[:]).then_inc(S.ldx, 16)
+
+    g.vector.memset(T.ones[:], 1.0).then_inc(S.fill, 1)
+    g.wait_ge(S.fill, 1)
+    g.affine_select(T.ident[:], T.ones[:], [[-1, DM]], AluOpType.is_equal, 0.0, 0, 1).then_inc(S.idn, 1)
+    g.wait_ge(S.ldw, 32)
+    for call in P["first"][r]:
+        push(own[:], own[:], S["aw%d" % r], call)
+    g.wait_ge(S.ldx, 32)
+    push(T.xd[:], T.xdp[:], S.axd, [(mate, P["near"](core, mate))])
+    pass_on()
+    g.wait_ge(S.spo, 1)
+    push(T.pout[:], T.pin[:], S.apin, [(mate, P["near"](core, mate))])
+    g.wait_ge(S.sent, total[0])
+
+    n_near = len(P["near"](mate, core))
+
+    te = g.tensor
+    te.wait_ge(S.ldw, 32)
+    te.wait_ge(S.ldx, 32)
+    te.wait_ge(S.idn, 1)
+    te.wait_ge(S.axd, n_near)
+
+    def front(k):
+        a, both = jobs[k]
+        w = T["wb%d" % a]
+        zb, ub, tb = T["zb%d" % (k % 2)], T["ub%d" % (k % 2)], T["tb%d" % (k % 2)]
+        if a != r:
+            te.wait_ge(S["aw%d" % a], P["arrive"][(core, a)])
+        te.matmul(zb[:, 0:TK], w[:, 0:DM], T.xd[:, 0:TK], True, True).then_inc(S["sz%d" % k], 1)
+        if both:
+            te.matmul(zb[:, TK:2 * TK], w[:, 0:DM], T.xdp[:, 0:TK], True, True).then_inc(S["sz%d" % k], 1)
+        te.transpose(tb[:, 0:DM], w[:, 0:DM], T.ident[:]).then_inc(S["st%d" % k], 1)
+        te.matmul(ub[:, 0:TK], w[:, DM:2 * DM], T.xd[:, TK:2 * TK], True, True).then_inc(S["su%d" % k], 1)
+        if both:
+            te.matmul(ub[:, TK:2 * TK], w[:, DM:2 * DM], T.xdp[:, TK:2 * TK], True, True).then_inc(S["su%d" % k], 1)
+
+    def back(k):
+        a, both = jobs[k]
+        te.wait_ge(S["sg%d" % k], 1)
+        te.wait_ge(S["sc%d" % k], 1)
+        wt, gg = T["wt%d" % k], T["gg%d" % k]
+        if both:
+            te.matmul(T.accp[:, 0:TK], wt[:], gg[:, TK:2 * TK], k == 0, k == nb - 1).then_inc(S.sdp, 1)
+        te.matmul(T.acco[:, 0:TK], wt[:], gg[:, 0:TK], k == 0, k == n - 1).then_inc(S.sdo, 1)
+
+    for lo, hi in ((0, nb), (nb, n)):
+        for k in range(lo, hi):
+            front(k)
+            if k > lo:
+                back(k - 1)
+        if hi > lo:
+            back(hi - 1)
+
+    for k in range(n):
+        g.scalar.wait_ge(S["st%d" % k], 1)
+        g.scalar.activation(T["wt%d" % k][:], T["tb%d" % (k % 2)][:, 0:DM],
+                            ActivationFunctionType.Copy).then_inc(S["sc%d" % k], 1)
+
+    ve = g.vector
+    for k in range(n):
+        a, both = jobs[k]
+        c = 2 if both else 1
+        mk, gg = T["mk%d" % k], T["gg%d" % k]
+        ve.wait_ge(S["sz%d" % k], c)
+        ve.tensor_scalar(mk[:, 0:c * TK], T["zb%d" % (k % 2)][:, 0:c * TK], 0.0, None,
+                         AluOpType.is_gt).then_inc(S["sm%d" % k], 1)
+        ve.wait_ge(S["su%d" % k], c)
+        ve.wait_ge(S["sm%d" % k], 1)
+        ve.tensor_tensor(gg[:, 0:c * TK], mk[:, 0:c * TK], T["ub%d" % (k % 2)][:, 0:c * TK],
+                         AluOpType.mult).then_inc(S["sg%d" % k], 1)
+        if k == nb - 1:
+            ve.wait_ge(S.sdp, nb)
+            ve.tensor_copy(T.pout[:], T.accp[:, 0:TK]).then_inc(S.spo, 1)
+    ve.wait_ge(S.sdo, n)
+    ve.wait_ge(S.apin, n_near)
+    ve.tensor_tensor(T.res[:], T.acco[:, 0:TK], T.pin[:], AluOpType.add).then_inc(S.sres, 1)
+
+    g.sync.wait_ge(S.sres, 1)
+    g.sync.dma_start(T.dx[:], T.res[:]).then_inc(S.sst, 16)
+    g.sync.wait_ge(S.sst, 16)

@@ -78,13 +78,18 @@ def _plan(cores, topo):
         calls = []
         if through:
             gate = cores[partner[a]]
-            es = near(ca, gate)
-            calls.append([(gate, es)])
-            arrive[(gate, a)] = len(es)
-            sh = _split(far(gate), len(through))
-            relay.setdefault(gate, []).append((a, [(cores[m], sh[i]) for i, m in enumerate(through)]))
-            for i, m in enumerate(through):
-                arrive[(cores[m], a)] = len(sh[i])
+            idle = [c for c in range(topo.CHIPS * topo.CORES_PER_CHIP)
+                    if topo.chip(c) == topo.chip(ca) and c not in cores and topo.die(c) == topo.die(ca)
+                    and all(topo.may_write(c, cores[m]) for m in through)][0]
+            mine = [m for m in through if topo.die(cores[m]) == topo.die(gate)]
+            parts = [(idle, far(ca), [m for m in through if m not in mine]), (gate, near(ca, gate), mine)]
+            for via, es, dests in parts:
+                calls.append([(via, es)])
+                arrive[(via, a)] = len(es)
+                sh = _split(far(via), len(dests))
+                relay.setdefault(via, []).append((a, [(cores[m], sh[i]) for i, m in enumerate(dests)]))
+                for i, m in enumerate(dests):
+                    arrive[(cores[m], a)] = len(sh[i])
         if straight:
             sh = _split(far(ca), len(straight))
             calls.append([(cores[h], sh[i]) for i, h in enumerate(straight)])

@@ -8,7 +8,8 @@ DM = 128
 SCRATCH = {
     "xd": ("sbuf", [128, 2 * TK], "bfloat16"),
     "xdp": ("sbuf", [128, 2 * TK], "bfloat16"),
-    "ones": ("sbuf", [128, DM], "bfloat16"),
+    "idxo": ("sbuf", [128, DM], "bfloat16"),
+    "idx": ("sbuf", [128, DM], "bfloat16"),
     "ident": ("sbuf", [128, DM], "bfloat16"),
     "pout": ("sbuf", [128, TK], "bfloat16"),
     "pin": ("sbuf", [128, TK], "bfloat16"),
@@ -18,7 +19,7 @@ SCRATCH = {
     "tb0": ("psum", [128, 1024], "bfloat16"), "tb1": ("psum", [128, 1024], "bfloat16"),
     "acco": ("psum", [128, 512], "float32"), "accp": ("psum", [128, 512], "float32"),
 }
-SEMAPHORES = ["ldw", "ldx", "fill", "idn", "sent", "axd", "apin", "spo", "sdo", "sdp", "sres", "sst"]
+SEMAPHORES = ["ldw", "ldx", "sio", "aid", "idn", "sent", "axd", "apin", "spo", "sdo", "sdp", "sres", "sst"]
 for _k in range(NR):
     SCRATCH["wb%d" % _k] = ("sbuf", [128, 2 * DM], "bfloat16")
     SCRATCH["wt%d" % _k] = ("sbuf", [128, DM], "bfloat16")
@@ -96,12 +97,24 @@ def _plan(cores, topo):
             for i, h in enumerate(straight):
                 arrive[(cores[h], a)] = len(sh[i])
         first[a] = calls
+    makers = dict((r, [cores[partner[r]]]) for r in range(n))
+    for via in sorted(relay):
+        if via not in cores:
+            mem = on[topo.chip(via)]
+            makers[min(mem, key=lambda m: (topo.die(cores[m]) != topo.die(via), m))].append(via)
+    feed, fed = {}, {}
+    for r in range(n):
+        w = DM // len(makers[r])
+        for i, s in enumerate(makers[r]):
+            feed[s] = (cores[r], i * w, w, far(s))
+        fed[r] = sum(len(far(s)) for s in makers[r])
     jobs = {}
     for r in range(n):
         me = topo.chip(cores[r])
         sh = sorted(shared[r], key=lambda a: (not topo.same_plane(topo.chip(cores[a]), me), a))
         jobs[r] = [(r, True)] + [(a, True) for a in sh] + [(a, False) for a in sorted(late[r])]
-    return {"jobs": jobs, "first": first, "relay": relay, "arrive": arrive, "partner": partner, "near": near}
+    return {"jobs": jobs, "first": first, "relay": relay, "arrive": arrive, "partner": partner, "near": near,
+            "feed": feed, "fed": fed}
 
 
 def rank_program(g, core, T, topo):
@@ -135,7 +148,14 @@ def rank_program(g, core, T, topo):
             buf = T["wb%d" % a]
             push(buf[:], buf[:], S["aw%d" % a], targets)
 
+    def index_columns():
+        d, off, w, es = P["feed"][core]
+        g.iota(T.idxo[:, 0:w], [[-1, w]], -off, 1, allow_small_or_imprecise_dtypes=True).then_inc(S.sio, 1)
+        g.wait_ge(S.sio, 1)
+        push(T.idxo[:, 0:w], T.idx[:, off:off + w], S.aid, [(d, es)])
+
     if r is None:
+        index_columns()
         pass_on()
         g.wait_ge(S.sent, total[0])
         return
@@ -151,9 +171,10 @@ def rank_program(g, core, T, topo):
     g.sync.dma_start(T.xd[:, 0:TK], T.x[:]).then_inc(S.ldx, 16)
     g.scalar.dma_start(T.xd[:, TK:2 * TK], T.dy[:]).then_inc(S.ldx, 16)
 
-    g.vector.memset(T.ones[:], 1.0).then_inc(S.fill, 1)
-    g.wait_ge(S.fill, 1)
-    g.affine_select(T.ident[:], T.ones[:], [[-1, DM]], AluOpType.is_equal, 0.0, 0, 1).then_inc(S.idn, 1)
+    def wide(c, d):
+        return P["near"](c, d) if P["relay"].get(c) else _bits(topo.mask(c, d))
+
+    index_columns()
     g.wait_ge(S.ldw, 32)
     for call in P["first"][r]:
         push(own[:], own[:], S["aw%d" % r], call)
@@ -161,16 +182,15 @@ def rank_program(g, core, T, topo):
     push(T.xd[:], T.xdp[:], S.axd, [(mate, P["near"](core, mate))])
     pass_on()
     g.wait_ge(S.spo, 1)
-    push(T.pout[:], T.pin[:], S.apin, [(mate, P["near"](core, mate))])
+    push(T.pout[:], T.pin[:], S.apin, [(mate, wide(core, mate))])
     g.wait_ge(S.sent, total[0])
 
     n_near = len(P["near"](mate, core))
+    n_pin = len(wide(mate, core))
 
     te = g.tensor
     te.wait_ge(S.ldw, 32)
     te.wait_ge(S.ldx, 32)
-    te.wait_ge(S.idn, 1)
-    te.wait_ge(S.axd, n_near)
 
     def front(k):
         a, both = jobs[k]
@@ -179,6 +199,14 @@ def rank_program(g, core, T, topo):
         if a != r:
             te.wait_ge(S["aw%d" % a], P["arrive"][(core, a)])
         te.matmul(zb[:, 0:TK], w[:, 0:DM], T.xd[:, 0:TK], True, True).then_inc(S["sz%d" % k], 1)
+        if k == 0:
+            te.matmul(ub[:, 0:TK], w[:, DM:2 * DM], T.xd[:, TK:2 * TK], True, True).then_inc(S["su%d" % k], 1)
+            te.wait_ge(S.axd, n_near)
+            te.matmul(zb[:, TK:2 * TK], w[:, 0:DM], T.xdp[:, 0:TK], True, True).then_inc(S["sz%d" % k], 1)
+            te.matmul(ub[:, TK:2 * TK], w[:, DM:2 * DM], T.xdp[:, TK:2 * TK], True, True).then_inc(S["su%d" % k], 1)
+            te.wait_ge(S.idn, 1)
+            te.transpose(tb[:, 0:DM], w[:, 0:DM], T.ident[:]).then_inc(S["st%d" % k], 1)
+            return
         if both:
             te.matmul(zb[:, TK:2 * TK], w[:, 0:DM], T.xdp[:, 0:TK], True, True).then_inc(S["sz%d" % k], 1)
         te.transpose(tb[:, 0:DM], w[:, 0:DM], T.ident[:]).then_inc(S["st%d" % k], 1)
@@ -209,6 +237,8 @@ def rank_program(g, core, T, topo):
                             ActivationFunctionType.Copy).then_inc(S["sc%d" % k], 1)
 
     ve = g.vector
+    ve.wait_ge(S.aid, P["fed"][r])
+    ve.tensor_scalar(T.ident[:], T.idx[:], 0.0, None, AluOpType.is_equal).then_inc(S.idn, 1)
     for k in range(n):
         a, both = jobs[k]
         c = 2 if both else 1
@@ -224,7 +254,7 @@ def rank_program(g, core, T, topo):
             ve.wait_ge(S.sdp, nb)
             ve.tensor_copy(T.pout[:], T.accp[:, 0:TK]).then_inc(S.spo, 1)
     ve.wait_ge(S.sdo, n)
-    ve.wait_ge(S.apin, n_near)
+    ve.wait_ge(S.apin, n_pin)
     ve.tensor_tensor(T.res[:], T.acco[:, 0:TK], T.pin[:], AluOpType.add).then_inc(S.sres, 1)
 
     g.sync.wait_ge(S.sres, 1)

from concourse.bass import DstId, RemoteDMATransfer
from concourse.mybir import AluOpType, ActivationFunctionType

NR = 6
TK = 64
DM = 128

SCRATCH = {
    "xd": ("sbuf", [128, 2 * TK], "bfloat16"),
    "xdp": ("sbuf", [128, 2 * TK], "bfloat16"),
    "idxo": ("sbuf", [128, DM], "bfloat16"),
    "idx": ("sbuf", [128, DM], "bfloat16"),
    "ident": ("sbuf", [128, DM], "bfloat16"),
    "pout": ("sbuf", [128, TK], "bfloat16"),
    "pin": ("sbuf", [128, TK], "bfloat16"),
    "res": ("sbuf", [128, TK], "bfloat16"),
    "zb0": ("psum", [128, 512], "float32"), "zb1": ("psum", [128, 512], "float32"),
    "ub0": ("psum", [128, 512], "float32"), "ub1": ("psum", [128, 512], "float32"),
    "tb0": ("psum", [128, 1024], "bfloat16"), "tb1": ("psum", [128, 1024], "bfloat16"),
    "acco": ("psum", [128, 512], "float32"), "accp": ("psum", [128, 512], "float32"),
}
SEMAPHORES = ["ldw", "ldx", "sio", "aid", "idn", "sent", "axd", "apin", "spo", "sdo", "sdp", "sres", "sst"]
for _k in range(NR):
    SCRATCH["wb%d" % _k] = ("sbuf", [128, 2 * DM], "bfloat16")
    SCRATCH["wt%d" % _k] = ("sbuf", [128, DM], "bfloat16")
    SCRATCH["mk%d" % _k] = ("sbuf", [128, 2 * TK], "bfloat16")
    SCRATCH["gg%d" % _k] = ("sbuf", [128, 2 * TK], "bfloat16")
    SEMAPHORES += ["aw%d" % _k, "sz%d" % _k, "su%d" % _k, "st%d" % _k, "sm%d" % _k, "sg%d" % _k, "sc%d" % _k]


def _bits(m):
    return [i for i in range(m.bit_length()) if (m >> i) & 1]


def _mask(es):
    return sum(1 << i for i in es)


def _split(es, k):
    per = 1
    while per * 2 * k <= len(es):
        per *= 2
    return [es[i * per:(i + 1) * per] for i in range(k)]


def _plan(cores, topo):
    n = len(cores)
    chips = sorted(set(topo.chip(c) for c in cores))
    on = dict((ch, [r for r in range(n) if topo.chip(cores[r]) == ch]) for ch in chips)

    def far(c):
        d = [x for x in cores if topo.chip(x) != topo.chip(c)][0]
        return _bits(topo.mask(c, d))

    def near(c, d):
        every = _bits(topo.mask(c, d))
        only = [e for e in every if e not in far(c)]
        return only or every

    partner = dict((r, [p for p in on[topo.chip(cores[r])] if p != r][0]) for r in range(n))
    shared = dict((r, []) for r in range(n))
    late = dict((r, []) for r in range(n))
    first, relay, arrive = {}, {}, {}
    for a in reversed(range(n)):
        ca = cores[a]
        straight, through = [], []
        for ch in chips:
            if ch == topo.chip(ca):
                continue
            mem = on[ch]
            if all(topo.may_write(ca, cores[m]) for m in mem):
                h = min(mem, key=lambda m: (len(shared[m]), topo.die(cores[m]) != topo.die(ca), m))
                shared[h].append(a)
                straight.append(h)
            else:
                through += mem
                for m in mem:
                    late[m].append(a)
        calls = []
        if through:
            gate = cores[partner[a]]
            idle = [c for c in range(topo.CHIPS * topo.CORES_PER_CHIP)
                    if topo.chip(c) == topo.chip(ca) and c not in cores and topo.die(c) == topo.die(ca)
                    and all(topo.may_write(c, cores[m]) for m in through)][0]
            mine = [m for m in through if topo.die(cores[m]) == topo.die(gate)]
            parts = [(idle, far(ca), [m for m in through if m not in mine]), (gate, near(ca, gate), mine)]
            for via, es, dests in parts:
                calls.append([(via, es)])
                arrive[(via, a)] = len(es)
                sh = _split(far(via), len(dests))
                relay.setdefault(via, []).append((a, [(cores[m], sh[i]) for i, m in enumerate(dests)]))
                for i, m in enumerate(dests):
                    arrive[(cores[m], a)] = len(sh[i])
        if straight:
            sh = _split(far(ca), len(straight))
            calls.append([(cores[h], sh[i]) for i, h in enumerate(straight)])
            for i, h in enumerate(straight):
                arrive[(cores[h], a)] = len(sh[i])
        first[a] = calls
    makers = dict((r, [cores[partner[r]]]) for r in range(n))
    for via in sorted(relay):
        if via not in cores:
            mem = on[topo.chip(via)]
            makers[min(mem, key=lambda m: (topo.die(cores[m]) != topo.die(via), m))].append(via)
    feed, fed = {}, {}
    for r in range(n):
        w = DM // len(makers[r])
        for i, s in enumerate(makers[r]):
            feed[s] = (cores[r], i * w, w, far(s))
        fed[r] = sum(len(far(s)) for s in makers[r])
    jobs = {}
    for r in range(n):
        me = topo.chip(cores[r])
        sh = sorted(shared[r], key=lambda a: (not topo.same_plane(topo.chip(cores[a]), me), a))
        jobs[r] = [(r, True)] + [(a, True) for a in sh] + [(a, False) for a in sorted(late[r])]
    return {"jobs": jobs, "first": first, "relay": relay, "arrive": arrive, "partner": partner, "near": near,
            "feed": feed, "fed": fed}


def rank_program(g, core, T, topo):
    cores = list(T.cores)
    P = _plan(cores, topo)
    S = T.sem
    r = T.rank_of(core)
    duties = P["relay"].get(core, [])
    if r is None and not duties:
        return
    total = [0]

    def push(src, dst, sem, targets):
        if len(targets) == 1:
            d, es = targets[0]
            rid, pid, se = topo.addr(d)
            g.remote_dma(out_ap=dst, in_ap=src, remote_sem=sem, local_sem=S.sent, pid=pid, routing_id=rid,
                         dma_engine_mask=_mask(es))
        else:
            trs = []
            for d, es in targets:
                rid, pid, se = topo.addr(d)
                trs.append(RemoteDMATransfer(dst_ids=[DstId(rid=rid, pnc=pid)], dma_engine_mask=_mask(es),
                                             remote_sem=sem, src=src, dst=dst))
            g.remote_dma_fused(trs, local_sem=S.sent)
        total[0] += sum(len(es) for d, es in targets)

    def pass_on():
        for a, targets in duties:
            g.wait_ge(S["aw%d" % a], P["arrive"][(core, a)])
            buf = T["wb%d" % a]
            push(buf[:], buf[:], S["aw%d" % a], targets)

    def index_columns():
        d, off, w, es = P["feed"][core]
        g.iota(T.idxo[:, 0:w], [[-1, w]], -off, 1, allow_small_or_imprecise_dtypes=True).then_inc(S.sio, 1)
        g.wait_ge(S.sio, 1)
        push(T.idxo[:, 0:w], T.idx[:, off:off + w], S.aid, [(d, es)])

    if r is None:
        index_columns()
        pass_on()
        g.wait_ge(S.sent, total[0])
        return

    own = T["wb%d" % r]
    mate = cores[P["partner"][r]]
    jobs = P["jobs"][r]
    n = len(jobs)
    nb = len([1 for a, both in jobs if both])

    g.sync.dma_start(own[:, 0:DM], T.w1[:]).then_inc(S.ldw, 16)
    g.scalar.dma_start(own[:, DM:2 * DM], T.w2t[:]).then_inc(S.ldw, 16)
    g.sync.dma_start(T.xd[:, 0:TK], T.x[:]).then_inc(S.ldx, 16)
    g.scalar.dma_start(T.xd[:, TK:2 * TK], T.dy[:]).then_inc(S.ldx, 16)

    def wide(c, d):
        return P["near"](c, d) if P["relay"].get(c) else _bits(topo.mask(c, d))

    index_columns()
    g.wait_ge(S.ldw, 32)
    for call in P["first"][r]:
        push(own[:], own[:], S["aw%d" % r], call)
    g.wait_ge(S.ldx, 32)
    push(T.xd[:], T.xdp[:], S.axd, [(mate, P["near"](core, mate))])
    pass_on()
    g.wait_ge(S.spo, 1)
    push(T.pout[:], T.pin[:], S.apin, [(mate, wide(core, mate))])
    g.wait_ge(S.sent, total[0])

    n_near = len(P["near"](mate, core))
    n_pin = len(wide(mate, core))

    te = g.tensor
    te.wait_ge(S.ldw, 32)
    te.wait_ge(S.ldx, 32)

    def front(k):
        a, both = jobs[k]
        w = T["wb%d" % a]
        zb, ub, tb = T["zb%d" % (k % 2)], T["ub%d" % (k % 2)], T["tb%d" % (k % 2)]
        if a != r:
            te.wait_ge(S["aw%d" % a], P["arrive"][(core, a)])
        te.matmul(zb[:, 0:TK], w[:, 0:DM], T.xd[:, 0:TK], True, True).then_inc(S["sz%d" % k], 1)
        if k == 0:
            te.matmul(ub[:, 0:TK], w[:, DM:2 * DM], T.xd[:, TK:2 * TK], True, True).then_inc(S["su%d" % k], 1)
            te.wait_ge(S.axd, n_near)
            te.matmul(zb[:, TK:2 * TK], w[:, 0:DM], T.xdp[:, 0:TK], True, True).then_inc(S["sz%d" % k], 1)
            te.matmul(ub[:, TK:2 * TK], w[:, DM:2 * DM], T.xdp[:, TK:2 * TK], True, True).then_inc(S["su%d" % k], 1)
            te.wait_ge(S.idn, 1)
            te.transpose(tb[:, 0:DM], w[:, 0:DM], T.ident[:]).then_inc(S["st%d" % k], 1)
            return
        if both:
            te.matmul(zb[:, TK:2 * TK], w[:, 0:DM], T.xdp[:, 0:TK], True, True).then_inc(S["sz%d" % k], 1)
        te.transpose(tb[:, 0:DM], w[:, 0:DM], T.ident[:]).then_inc(S["st%d" % k], 1)
        te.matmul(ub[:, 0:TK], w[:, DM:2 * DM], T.xd[:, TK:2 * TK], True, True).then_inc(S["su%d" % k], 1)
        if both:
            te.matmul(ub[:, TK:2 * TK], w[:, DM:2 * DM], T.xdp[:, TK:2 * TK], True, True).then_inc(S["su%d" % k], 1)

    def back(k):
        a, both = jobs[k]
        te.wait_ge(S["sg%d" % k], 1)
        te.wait_ge(S["sc%d" % k], 1)
        wt, gg = T["wt%d" % k], T["gg%d" % k]
        if both:
            te.matmul(T.accp[:, 0:TK], wt[:], gg[:, TK:2 * TK], k == 0, k == nb - 1).then_inc(S.sdp, 1)
        te.matmul(T.acco[:, 0:TK], wt[:], gg[:, 0:TK], k == 0, k == n - 1).then_inc(S.sdo, 1)

    for lo, hi in ((0, nb), (nb, n)):
        for k in range(lo, hi):
            front(k)
            if k > lo:
                back(k - 1)
        if hi > lo:
            back(hi - 1)

    for k in range(n):
        g.scalar.wait_ge(S["st%d" % k], 1)
        g.scalar.activation(T["wt%d" % k][:], T["tb%d" % (k % 2)][:, 0:DM],
                            ActivationFunctionType.Copy).then_inc(S["sc%d" % k], 1)

    ve = g.vector
    ve.wait_ge(S.aid, P["fed"][r])
    ve.tensor_scalar(T.ident[:], T.idx[:], 0.0, None, AluOpType.is_equal).then_inc(S.idn, 1)
    for k in range(n):
        a, both = jobs[k]
        c = 2 if both else 1
        mk, gg = T["mk%d" % k], T["gg%d" % k]
        ve.wait_ge(S["sz%d" % k], c)
        ve.tensor_scalar(mk[:, 0:c * TK], T["zb%d" % (k % 2)][:, 0:c * TK], 0.0, None,
                         AluOpType.is_gt).then_inc(S["sm%d" % k], 1)
        ve.wait_ge(S["su%d" % k], c)
        ve.wait_ge(S["sm%d" % k], 1)
        ve.tensor_tensor(gg[:, 0:c * TK], mk[:, 0:c * TK], T["ub%d" % (k % 2)][:, 0:c * TK],
                         AluOpType.mult).then_inc(S["sg%d" % k], 1)
        if k == nb - 1:
            ve.wait_ge(S.sdp, nb)
            ve.tensor_copy(T.pout[:], T.accp[:, 0:TK]).then_inc(S.spo, 1)
    ve.wait_ge(S.sdo, n)
    ve.wait_ge(S.apin, n_pin)
    ve.tensor_tensor(T.res[:], T.acco[:, 0:TK], T.pin[:], AluOpType.add).then_inc(S.sres, 1)

    g.sync.wait_ge(S.sres, 1)
    g.sync.dma_start(T.dx[:], T.res[:]).then_inc(S.sst, 16)
    g.sync.wait_ge(S.sst, 16)
